import numpy as np
import ml_dtypes


def mxq(x, axis, fmt="e4m3"):
    dtype, down = {"e4m3": (ml_dtypes.float8_e4m3fn, 7), "e5m2": (ml_dtypes.float8_e5m2, 14)}[fmt]
    v = np.moveaxis(np.asarray(x, np.float32).astype(ml_dtypes.bfloat16).astype(np.float64), axis, -1)
    blocks = v.reshape(v.shape[:-1] + (-1, 32))
    amax = np.abs(blocks).max(-1, keepdims=True)
    byte = np.maximum(np.where(amax > 0, np.frexp(amax)[1] - 1 + 127, 0) - down, 1)
    scale = np.exp2(byte - 127.0)
    codes = (blocks / scale).astype(np.float32).astype(dtype).astype(np.float64)
    return np.moveaxis((codes * scale).reshape(v.shape), -1, axis)


WIDE = False


def mx_kscale(k):
    if not WIDE:
        return np.ones(k)
    levels = np.array([10, -10, 5, -5, 0])
    if k % 512:
        return np.exp2(np.random.permutation(np.resize(levels, k // 32))).repeat(32)
    a = np.empty((k // 512, 16))
    for p in range(k // 512):
        a[p, :8] = np.random.permutation(np.resize(levels, 8))
        for g in range(8):
            far = levels[np.abs(levels - a[p, g]) >= 10]
            a[p, g + 8] = far[np.random.randint(len(far))]
    return np.exp2(a.ravel()).repeat(32)


def f64(x):
    return np.asarray(x).astype(np.float64)


def striped(idx):
    return np.tile(idx.reshape(-1, 16).T, (8, 1)).astype(np.uint16)


def unstriped(offs):
    return offs[:16].T.reshape(-1).astype(np.int64)


def pack_weight(w):
    k, n = w.shape
    w = f64(np.asarray(w, np.float32).astype(ml_dtypes.bfloat16)).reshape(k // 32, 32, n)
    amax = np.abs(w).max(1)
    byte = np.clip(np.where(amax > 0, np.frexp(amax)[1] - 1 + 127 - 7, 1), 1, 254)
    scaled = (w * np.exp2(127.0 - byte)[:, None, :]).reshape(k, n).astype(np.float32)
    words = np.ascontiguousarray(scaled.reshape(k // 512, 128, 4, n).transpose(0, 1, 3, 2)).astype(ml_dtypes.float8_e4m3fn).view(np.uint8)
    return words, np.ascontiguousarray(byte.astype(np.uint8).reshape(k // 512, 16, n))


def unpack_weight(words, scales):
    g, p, n, _ = words.shape
    vals = np.ascontiguousarray(words).view(ml_dtypes.float8_e4m3fn).astype(np.float64) * np.repeat(np.exp2(scales.astype(np.float64) - 127.0), 8, axis=1)[..., None]
    return vals.transpose(0, 1, 3, 2).reshape(g * 512, n)


def relu(v):
    return np.maximum(v, 0.0)


K, T, S, D, N = 1024, 2048, 1024, 4, 256


def setup_inputs():
    n = np.random.standard_normal
    s = mx_kscale(K)[:, None]
    packed_xT = pack_weight(n((K, T)) * s)
    return {
        "x_words": packed_xT[0],
        "x_scales": packed_xT[1],
        "w1": (n((K, N)) / np.sqrt(K) / s).astype(np.float32),
        "offs": striped(np.random.permutation(T)[:S]),
    }


def reference(x_words, x_scales, w1, offs):
    xq = unpack_weight(x_words, x_scales)[:, unstriped(offs)]
    y = mxq(f64(w1), 0, "e4m3").T @ xq
    rr = 0.5 * ((y) ** 2)
    ker = (relu(-0.4 * rr + 1.0)) ** 2
    dens = ker.reshape(len(ker), -1, D).sum(axis=2) + 0.6
    wy = ker * y
    cf = wy.reshape(len(wy), -1, D).sum(axis=2)
    return np.log(dens) - (0.3 * (((cf) ** 2) / dens))

@@ -1,0 +1,193 @@
+import math
+from contextlib import ExitStack
+
+import concourse.mybir as mybir
+from concourse.masks import make_identity
+
+K, T, S, D, N = 1024, 2048, 1024, 4, 256
+FLOPS = 2 * K * N * S
+
+F32 = mybir.dt.float32
+BF16 = mybir.dt.bfloat16
+I32 = mybir.dt.int32
+U32 = mybir.dt.uint32
+U16 = mybir.dt.uint16
+U8 = mybir.dt.uint8
+FP8X4 = mybir.dt.float8_e4m3fn_x4
+ACT = mybir.ActivationFunctionType
+ALU = mybir.AluOpType
+
+P = 128
+PASSES = K // 512
+HALVES = N // P
+CHUNKS = 4
+CW = S // CHUNKS
+CV = CW // D
+
+
+def tile_picked_ysph_col_p_kernel(tc, x_words, x_scales, w1, offs, out):
+    nc = tc.nc
+    with ExitStack() as ctx:
+        keep = ctx.enter_context(tc.tile_pool(name="keep", bufs=1))
+        ring = ctx.enter_context(tc.tile_pool(name="ring", bufs=2))
+        work = ctx.enter_context(tc.tile_pool(name="work", bufs=4))
+        y_psum = ctx.enter_context(tc.psum_pool(name="y_psum", bufs=3))
+        d_psum = ctx.enter_context(tc.psum_pool(name="d_psum", bufs=1))
+        c_psum = ctx.enter_context(tc.psum_pool(name="c_psum", bufs=2))
+
+        offsets = keep.tile([P, S // 16], U16, name="offsets")
+        nc.sync.dma_start(offsets[:], offs)
+
+        scale_table = keep.tile([P, T], U8, name="scale_table", align_bytes=64)
+        nc.vector.memset(scale_table[:].bitcast(I32), 0)
+        for q in range(4):
+            nc.gpsimd.dma_start(
+                out=scale_table[32 * q : 32 * q + 8, :].bitcast(I32),
+                in_=x_scales[:, 4 * q : 4 * q + 4, :].bitcast(I32),
+            )
+
+        word_table = [keep.tile([P, T], U32, name=f"word_table{g}", align_bytes=64) for g in range(PASSES)]
+        w_raw = [keep.tile([P, 4, N], F32, name=f"w_raw{g}") for g in range(PASSES)]
+
+        def load_words(g):
+            nc.sync.dma_start(
+                out=word_table[g][:].bitcast(I32),
+                in_=x_words[g].rearrange("p n t -> p (n t)").bitcast(I32),
+            )
+
+        load_words(0)
+        for g in range(PASSES):
+            nc.sync.dma_start(out=w_raw[g][:], in_=w1[512 * g : 512 * (g + 1), :].rearrange("(p j) m -> p j m", j=4))
+        load_words(1)
+
+        ones = keep.tile([P, P], F32, name="ones")
+        nc.vector.memset(ones[:], 1.0)
+        warm = keep.tile([P, 1], F32, name="warm")
+        nc.scalar.activation(warm[:], ones[:, 0:1], ACT.Abs_reciprocal_sqrt)
+        floor = keep.tile([P, P], F32, name="floor")
+        nc.vector.tensor_scalar(floor[:], ones[:], 0.6, None, ALU.mult)
+        ident = keep.tile([P, P], F32, name="ident")
+        make_identity(nc, ident[:])
+
+        x_codes = [[keep.tile([P, CW], U32, name=f"x_codes{g}_{c}", align_bytes=64) for c in range(CHUNKS)] for g in range(PASSES)]
+        x_planes = [ring.tile([P, CW], U8, name="x_planes", align_bytes=64) for c in range(CHUNKS)]
+
+        def piece(c):
+            return offsets[:, c * CW // 16 : (c + 1) * CW // 16]
+
+        def gather_words(g, c):
+            nc.vector.tensor_copy(x_codes[g][c][:], word_table[g][:].indirect(piece(c)))
+
+        for c in range(CHUNKS):
+            gather_words(0, c)
+
+        def gather_scales(c):
+            nc.vector.tensor_copy(x_planes[c][:], scale_table[:].indirect(piece(c)))
+
+        gather_scales(0)
+        gather_scales(1)
+
+        w_codes, w_planes = [], []
+        for g in range(PASSES):
+            grouped = keep.tile([P, N, 4], BF16, name=f"grouped{g}", align_bytes=64)
+            nc.scalar.copy(
+                out=grouped[:].rearrange("p (c i) t -> p c t i", i=4),
+                in_=w_raw[g][:].rearrange("p t (c i) -> p c t i", i=4),
+            )
+            codes = keep.tile([P, N], U32, name=f"w_codes{g}", align_bytes=64)
+            plane = keep.tile([P, N], U8, name=f"w_plane{g}", align_bytes=64)
+            nc.vector.quantize_mx(out=codes[:].bitcast(FP8X4), scales=plane[:], in_=grouped[:].rearrange("p m t -> p (m t)"))
+            w_codes.append(codes)
+            w_planes.append(plane)
+
+        st = [dict() for c in range(CHUNKS)]
+        early = CHUNKS - 1
+        dens_early = d_psum.tile([P, early, P], F32, name="dens_early")
+        dens_last = d_psum.tile([P, P], F32, name="dens_last")
+        term = keep.tile([P, CHUNKS, P], F32, name="term")
+        logd = keep.tile([P, CHUNKS, P], F32, name="logd")
+
+        def product(c):
+            if c >= 2:
+                gather_scales(c)
+            gather_words(1, c)
+            y = y_psum.tile([P, HALVES, CW], F32, name="y")
+            for h in range(HALVES):
+                cols = slice(h * P, (h + 1) * P)
+                for g in range(PASSES):
+                    nc.tensor.matmul_mx(
+                        out=y[:, h, :],
+                        lhsT=w_codes[g][:, cols].bitcast(FP8X4),
+                        lhsT_scale=w_planes[g][:, cols],
+                        rhs=x_codes[g][c][:].bitcast(FP8X4),
+                        rhs_scale=x_planes[c][4 * g : P, :],
+                        start=(g == 0),
+                        stop=(g == PASSES - 1),
+                    )
+            by_pair = y[:].rearrange("p h (v d) -> p d h v", d=D)
+            sq = work.tile([P, D, HALVES, CV], F32, name="sq")
+            nc.scalar.activation(sq[:], by_pair, ACT.Square, scale=math.sqrt(0.2))
+            st[c]["y"] = by_pair
+            st[c]["sq"] = sq
+
+        def weights(c):
+            sq = st[c]["sq"]
+            neg = work.tile([P, D, HALVES, CV], F32, name="neg")
+            nc.vector.tensor_scalar(neg[:], sq[:], 1.0, 1.0, ALU.min, ALU.subtract)
+            ker = work.tile([P, D, HALVES, CV], F32, name="ker")
+            nc.scalar.activation(ker[:], neg[:], ACT.Square)
+            wy = work.tile([P, D, HALVES, CV], F32, name="wy")
+            nc.vector.tensor_tensor(wy[:], ker[:], st[c]["y"], ALU.mult)
+            dens = dens_early[:, c, :] if c < early else dens_last[:]
+            if c == early:
+                nc.tensor.matmul(dens, lhsT=floor[:], rhs=ident[:], start=True, stop=False, is_transpose=True)
+            for d in range(D):
+                nc.tensor.matmul(dens, lhsT=ker[:, d].rearrange("p h v -> p (h v)"), rhs=ident[:], start=(d == 0 and c < early), stop=(d == D - 1), is_transpose=True)
+            cf = c_psum.tile([P, P], F32, name="cf")
+            for d in range(D):
+                nc.tensor.matmul(cf[:], lhsT=wy[:, d].rearrange("p h v -> p (h v)"), rhs=ident[:], start=(d == 0), stop=(d == D - 1), is_transpose=True)
+            st[c]["dens"] = dens
+            st[c]["cf"] = cf
+
+        def gradient_term(c):
+            dens, cf = st[c]["dens"], st[c]["cf"]
+            inv = work.tile([P, P], F32, name="inv")
+            scaled = work.tile([P, P], F32, name="scaled")
+            if c < early:
+                nc.scalar.activation(inv[:], dens, ACT.Abs_reciprocal_sqrt, bias=floor[:, 0:1])
+                nc.vector.tensor_tensor(scaled[:], cf[:], inv[:], ALU.mult)
+                nc.vector.scalar_tensor_tensor(term[:, c, :], scaled[:], -0.3, scaled[:], ALU.mult, ALU.mult)
+            else:
+                nc.vector.reciprocal(inv[:], dens)
+                nc.vector.tensor_tensor(scaled[:], cf[:], inv[:], ALU.mult)
+                nc.vector.scalar_tensor_tensor(term[:, c, :], scaled[:], -0.3, cf[:], ALU.mult, ALU.mult)
+
+        def turn_back(c0, c1):
+            back = y_psum.tile([P, c1 - c0, HALVES, CV], F32, name="y")
+            for c in range(c0, c1):
+                dst = back[:, c - c0].rearrange("p h v -> p (h v)")
+                nc.tensor.matmul(dst, lhsT=logd[:, c, :], rhs=ident[:], start=True, stop=False, is_transpose=True)
+                nc.tensor.matmul(dst, lhsT=term[:, c, :], rhs=ident[:], start=False, stop=True, is_transpose=True)
+            return back
+
+        def store(c0, c1, back, copy):
+            res = keep.tile([P, HALVES, c1 - c0, CV], F32, name=f"res{c0}")
+            copy(out=res[:], in_=back[:].rearrange("p c h v -> p h c v"))
+            nc.sync.dma_start(
+                out=out.rearrange("(h p) v -> p h v", p=P)[:, :, c0 * CV : c1 * CV],
+                in_=res[:].rearrange("p h c v -> p h (c v)"),
+            )
+
+        for step in range(CHUNKS + 2):
+            if step < CHUNKS:
+                product(step)
+            if 0 <= step - 1 < CHUNKS:
+                weights(step - 1)
+            if 0 <= step - 2 < CHUNKS:
+                gradient_term(step - 2)
+        nc.scalar.activation(logd[:, 0:early, :], dens_early[:], ACT.Ln, bias=floor[:, 0:1])
+        nc.scalar.activation(logd[:, early, :], dens_last[:], ACT.Ln)
+        back_early = turn_back(0, early)
+        back_last = turn_back(early, CHUNKS)
+        store(0, early, back_early, nc.scalar.copy)
+        store(early, CHUNKS, back_last, nc.vector.tensor_copy)

@@ -20,18 +20,18 @@ ALU = mybir.AluOpType
 P = 128
 PASSES = K // 512
 HALVES = N // P
-CHUNKS = 4
-CW = S // CHUNKS
-CV = CW // D
+PIECE = P * D
+PIECES = S // PIECE
+CHUNKS = PIECES * HALVES
+LAST = CHUNKS - 1
 
 
 def tile_picked_ysph_col_p_kernel(tc, x_words, x_scales, w1, offs, out):
     nc = tc.nc
     with ExitStack() as ctx:
         keep = ctx.enter_context(tc.tile_pool(name="keep", bufs=1))
-        ring = ctx.enter_context(tc.tile_pool(name="ring", bufs=2))
-        work = ctx.enter_context(tc.tile_pool(name="work", bufs=4))
-        y_psum = ctx.enter_context(tc.psum_pool(name="y_psum", bufs=3))
+        work = ctx.enter_context(tc.tile_pool(name="work", bufs=CHUNKS))
+        y_psum = ctx.enter_context(tc.psum_pool(name="y_psum", bufs=CHUNKS))
         d_psum = ctx.enter_context(tc.psum_pool(name="d_psum", bufs=1))
         c_psum = ctx.enter_context(tc.psum_pool(name="c_psum", bufs=2))
 
@@ -39,7 +39,7 @@ def tile_picked_ysph_col_p_kernel(tc, x_words, x_scales, w1, offs, out):
         nc.sync.dma_start(offsets[:], offs)
 
         scale_table = keep.tile([P, T], U8, name="scale_table", align_bytes=64)
-        nc.vector.memset(scale_table[:].bitcast(I32), 0)
+        nc.gpsimd.memset(scale_table[:].bitcast(I32), 0)
         for q in range(4):
             nc.gpsimd.dma_start(
                 out=scale_table[32 * q : 32 * q + 8, :].bitcast(I32),
@@ -67,28 +67,24 @@ def tile_picked_ysph_col_p_kernel(tc, x_words, x_scales, w1, offs, out):
         floor = keep.tile([P, P], F32, name="floor")
         nc.vector.tensor_scalar(floor[:], ones[:], 0.6, None, ALU.mult)
         ident = keep.tile([P, P], F32, name="ident")
-        make_identity(nc, ident[:])
+        nc.vector.memset(ident[:], 0.0)
+        make_identity(nc, ident[:], nomemset=True)
 
-        x_codes = [[keep.tile([P, CW], U32, name=f"x_codes{g}_{c}", align_bytes=64) for c in range(CHUNKS)] for g in range(PASSES)]
-        x_planes = [ring.tile([P, CW], U8, name="x_planes", align_bytes=64) for c in range(CHUNKS)]
+        x_codes = [[keep.tile([P, PIECE], U32, name=f"x_codes{g}_{j}", align_bytes=64) for j in range(PIECES)] for g in range(PASSES)]
+        x_planes = [keep.tile([P, PIECE], U8, name="x_planes", align_bytes=64) for j in range(PIECES)]
 
-        def piece(c):
-            return offsets[:, c * CW // 16 : (c + 1) * CW // 16]
+        def piece(j):
+            return offsets[:, j * PIECE // 16 : (j + 1) * PIECE // 16]
 
-        def gather_words(g, c):
-            nc.vector.tensor_copy(x_codes[g][c][:], word_table[g][:].indirect(piece(c)))
+        def gather_words(g, j):
+            nc.vector.tensor_copy(x_codes[g][j][:], word_table[g][:].indirect(piece(j)))
 
-        for c in range(CHUNKS):
-            gather_words(0, c)
-
-        def gather_scales(c):
-            nc.vector.tensor_copy(x_planes[c][:], scale_table[:].indirect(piece(c)))
-
-        gather_scales(0)
-        gather_scales(1)
+        def gather_scales(j):
+            nc.vector.tensor_copy(x_planes[j][:], scale_table[:].indirect(piece(j)))
 
         w_codes, w_planes = [], []
-        for g in range(PASSES):
+
+        def quantise_weights(g):
             grouped = keep.tile([P, N, 4], BF16, name=f"grouped{g}", align_bytes=64)
             nc.scalar.copy(
                 out=grouped[:].rearrange("p (c i) t -> p c t i", i=4),
@@ -100,94 +96,121 @@ def tile_picked_ysph_col_p_kernel(tc, x_words, x_scales, w1, offs, out):
             w_codes.append(codes)
             w_planes.append(plane)
 
-        st = [dict() for c in range(CHUNKS)]
-        early = CHUNKS - 1
-        dens_early = d_psum.tile([P, early, P], F32, name="dens_early")
-        dens_last = d_psum.tile([P, P], F32, name="dens_last")
-        term = keep.tile([P, CHUNKS, P], F32, name="term")
-        logd = keep.tile([P, CHUNKS, P], F32, name="logd")
+        y = [y_psum.tile([P, PIECE], F32, name="y") for c in range(CHUNKS)]
 
-        def product(c):
-            if c >= 2:
-                gather_scales(c)
-            gather_words(1, c)
-            y = y_psum.tile([P, HALVES, CW], F32, name="y")
-            for h in range(HALVES):
-                cols = slice(h * P, (h + 1) * P)
-                for g in range(PASSES):
-                    nc.tensor.matmul_mx(
-                        out=y[:, h, :],
-                        lhsT=w_codes[g][:, cols].bitcast(FP8X4),
-                        lhsT_scale=w_planes[g][:, cols],
-                        rhs=x_codes[g][c][:].bitcast(FP8X4),
-                        rhs_scale=x_planes[c][4 * g : P, :],
-                        start=(g == 0),
-                        stop=(g == PASSES - 1),
-                    )
-            by_pair = y[:].rearrange("p h (v d) -> p d h v", d=D)
-            sq = work.tile([P, D, HALVES, CV], F32, name="sq")
-            nc.scalar.activation(sq[:], by_pair, ACT.Square, scale=math.sqrt(0.2))
-            st[c]["y"] = by_pair
-            st[c]["sq"] = sq
-
-        def weights(c):
-            sq = st[c]["sq"]
-            neg = work.tile([P, D, HALVES, CV], F32, name="neg")
-            nc.vector.tensor_scalar(neg[:], sq[:], 1.0, 1.0, ALU.min, ALU.subtract)
-            ker = work.tile([P, D, HALVES, CV], F32, name="ker")
-            nc.scalar.activation(ker[:], neg[:], ACT.Square)
-            wy = work.tile([P, D, HALVES, CV], F32, name="wy")
-            nc.vector.tensor_tensor(wy[:], ker[:], st[c]["y"], ALU.mult)
-            dens = dens_early[:, c, :] if c < early else dens_last[:]
-            if c == early:
-                nc.tensor.matmul(dens, lhsT=floor[:], rhs=ident[:], start=True, stop=False, is_transpose=True)
-            for d in range(D):
-                nc.tensor.matmul(dens, lhsT=ker[:, d].rearrange("p h v -> p (h v)"), rhs=ident[:], start=(d == 0 and c < early), stop=(d == D - 1), is_transpose=True)
-            cf = c_psum.tile([P, P], F32, name="cf")
-            for d in range(D):
-                nc.tensor.matmul(cf[:], lhsT=wy[:, d].rearrange("p h v -> p (h v)"), rhs=ident[:], start=(d == 0), stop=(d == D - 1), is_transpose=True)
-            st[c]["dens"] = dens
-            st[c]["cf"] = cf
-
-        def gradient_term(c):
-            dens, cf = st[c]["dens"], st[c]["cf"]
-            inv = work.tile([P, P], F32, name="inv")
-            scaled = work.tile([P, P], F32, name="scaled")
-            if c < early:
-                nc.scalar.activation(inv[:], dens, ACT.Abs_reciprocal_sqrt, bias=floor[:, 0:1])
-                nc.vector.tensor_tensor(scaled[:], cf[:], inv[:], ALU.mult)
-                nc.vector.scalar_tensor_tensor(term[:, c, :], scaled[:], -0.3, scaled[:], ALU.mult, ALU.mult)
-            else:
-                nc.vector.reciprocal(inv[:], dens)
-                nc.vector.tensor_tensor(scaled[:], cf[:], inv[:], ALU.mult)
-                nc.vector.scalar_tensor_tensor(term[:, c, :], scaled[:], -0.3, cf[:], ALU.mult, ALU.mult)
-
-        def turn_back(c0, c1):
-            back = y_psum.tile([P, c1 - c0, HALVES, CV], F32, name="y")
-            for c in range(c0, c1):
-                dst = back[:, c - c0].rearrange("p h v -> p (h v)")
-                nc.tensor.matmul(dst, lhsT=logd[:, c, :], rhs=ident[:], start=True, stop=False, is_transpose=True)
-                nc.tensor.matmul(dst, lhsT=term[:, c, :], rhs=ident[:], start=False, stop=True, is_transpose=True)
-            return back
-
-        def store(c0, c1, back, copy):
-            res = keep.tile([P, HALVES, c1 - c0, CV], F32, name=f"res{c0}")
-            copy(out=res[:], in_=back[:].rearrange("p c h v -> p h c v"))
-            nc.sync.dma_start(
-                out=out.rearrange("(h p) v -> p h v", p=P)[:, :, c0 * CV : c1 * CV],
-                in_=res[:].rearrange("p h c v -> p h (c v)"),
+        def product(c, g):
+            j, h = divmod(c, HALVES)
+            cols = slice(h * P, (h + 1) * P)
+            nc.tensor.matmul_mx(
+                out=y[c][:],
+                lhsT=w_codes[g][:, cols].bitcast(FP8X4),
+                lhsT_scale=w_planes[g][:, cols],
+                rhs=x_codes[g][j][:].bitcast(FP8X4),
+                rhs_scale=x_planes[j][4 * g : P, :],
+                start=(g == 0),
+                stop=(g == PASSES - 1),
             )
 
-        for step in range(CHUNKS + 2):
-            if step < CHUNKS:
-                product(step)
-            if 0 <= step - 1 < CHUNKS:
-                weights(step - 1)
-            if 0 <= step - 2 < CHUNKS:
-                gradient_term(step - 2)
-        nc.scalar.activation(logd[:, 0:early, :], dens_early[:], ACT.Ln, bias=floor[:, 0:1])
-        nc.scalar.activation(logd[:, early, :], dens_last[:], ACT.Ln)
-        back_early = turn_back(0, early)
-        back_last = turn_back(early, CHUNKS)
-        store(0, early, back_early, nc.scalar.copy)
-        store(early, CHUNKS, back_last, nc.vector.tensor_copy)
+        for j in range(PIECES):
+            gather_words(0, j)
+        for g in range(PASSES):
+            quantise_weights(g)
+        for j in range(PIECES):
+            gather_scales(j)
+            gather_words(1, j)
+            for h in range(HALVES):
+                for g in range(PASSES):
+                    product(j * HALVES + h, g)
+
+        dens_early = d_psum.tile([P, LAST, P], F32, name="dens_early")
+        dens_last = d_psum.tile([P, P], F32, name="dens_last")
+        by_pair = [y[c][:].rearrange("p (v d) -> p d v", d=D) for c in range(CHUNKS)]
+        sq, ker, cf, inv, back, term = {}, {}, {}, {}, {}, {}
+
+        def turn(dst, src, start, stop):
+            nc.tensor.matmul(dst, lhsT=src, rhs=ident[:], start=start, stop=stop, is_transpose=True)
+
+        def square(c):
+            sq[c] = work.tile([P, D, P], F32, name="sq")
+            nc.scalar.activation(sq[c][:], by_pair[c], ACT.Square, scale=math.sqrt(0.2))
+
+        def weights(c):
+            neg = work.tile([P, D, P], F32, name="neg") if c < LAST else keep.tile([P, D, P], F32, name="late")
+            if c == 0:
+                nc.scalar.activation(neg[:], sq[c][:], ACT.Relu, scale=-1.0, bias=ones[:, 0:1])
+            else:
+                nc.vector.tensor_scalar(neg[:], sq[c][:], 1.0, 1.0, ALU.min, ALU.subtract)
+            ker[c] = work.tile([P, D, P], F32, name="ker")
+            nc.scalar.activation(ker[c][:], neg[:], ACT.Square)
+            if c < LAST:
+                for d in range(D):
+                    turn(dens_early[:, c, :], ker[c][:, d, :], d == 0, d == D - 1)
+            else:
+                turn(dens_last[:], floor[:], True, False)
+                for d in range(D):
+                    turn(dens_last[:], ker[c][:, d, :], False, d == D - 1)
+
+        def gradient(c):
+            wy = work.tile([P, D, P], F32, name="wy")
+            nc.vector.tensor_tensor(wy[:], ker[c][:], by_pair[c], ALU.mult)
+            cf[c] = c_psum.tile([P, P], F32, name="cf")
+            for d in range(D):
+                turn(cf[c][:], wy[:, d, :], d == 0, d == D - 1)
+
+        def inverse(c):
+            inv[c] = work.tile([P, P], F32, name="inv")
+            if c < LAST:
+                nc.scalar.activation(inv[c][:], dens_early[:, c, :], ACT.Abs_reciprocal_sqrt, bias=floor[:, 0:1])
+            else:
+                nc.vector.reciprocal(inv[c][:], dens_last[:])
+
+        def gradient_term(c):
+            scaled = work.tile([P, P], F32, name="scaled")
+            term[c] = work.tile([P, P], F32, name="term")
+            nc.vector.tensor_tensor(scaled[:], cf[c][:], inv[c][:], ALU.mult)
+            if c < LAST:
+                nc.vector.scalar_tensor_tensor(term[c][:], scaled[:], -0.3, scaled[:], ALU.mult, ALU.mult)
+            else:
+                nc.vector.scalar_tensor_tensor(term[c][:], scaled[:], 0.3, cf[c][:], ALU.mult, ALU.mult)
+
+        square(0)
+        square(1)
+        weights(0)
+        square(2)
+        weights(1)
+        square(3)
+        gradient(0)
+        inverse(0)
+        weights(2)
+        weights(3)
+        gradient(1)
+        inverse(1)
+        inverse(2)
+        gradient_term(0)
+        gradient(2)
+        gradient_term(1)
+        gradient(3)
+        inverse(3)
+        gradient_term(3)
+        gradient_term(2)
+        for c in range(CHUNKS):
+            back[c] = y_psum.tile([P, P], F32, name="y")
+        for c in range(LAST):
+            turn(back[c][:], term[c][:], True, False)
+
+        logd = keep.tile([P, CHUNKS, P], F32, name="late")
+        nc.scalar.activation(logd[:, 0:LAST, :], dens_early[:], ACT.Ln, bias=floor[:, 0:1])
+        nc.scalar.activation(logd[:, LAST, :], inv[LAST][:], ACT.Ln)
+        turn(back[LAST][:], logd[:, LAST, :], True, False)
+        turn(back[LAST][:], term[LAST][:], False, True)
+        for c in range(LAST):
+            turn(back[c][:], logd[:, c, :], False, True)
+
+        rows = out.rearrange("(h p) v -> p h v", p=P)
+        res = [keep.tile([P, HALVES, P], F32, name=f"res{j}") for j in range(PIECES)]
+        nc.vector.tensor_scalar(res[PIECES - 1][:, HALVES - 1, :], back[LAST][:], -1.0, None, ALU.mult)
+        for c in range(LAST):
+            j, h = divmod(c, HALVES)
+            nc.scalar.copy(out=res[j][:, h, :], in_=back[c][:])
+        for j in range(PIECES):
+            nc.sync.dma_start(out=rows[:, :, j * P : (j + 1) * P], in_=res[j][:])

@@ -31,9 +31,8 @@ def tile_picked_ysph_col_p_kernel(tc, x_words, x_scales, w1, offs, out):
     with ExitStack() as ctx:
         keep = ctx.enter_context(tc.tile_pool(name="keep", bufs=1))
         work = ctx.enter_context(tc.tile_pool(name="work", bufs=CHUNKS))
-        y_psum = ctx.enter_context(tc.psum_pool(name="y_psum", bufs=CHUNKS))
+        y_psum = ctx.enter_context(tc.psum_pool(name="y_psum", bufs=CHUNKS + 2))
         d_psum = ctx.enter_context(tc.psum_pool(name="d_psum", bufs=1))
-        c_psum = ctx.enter_context(tc.psum_pool(name="c_psum", bufs=2))
 
         offsets = keep.tile([P, S // 16], U16, name="offsets")
         nc.sync.dma_start(offsets[:], offs)
@@ -41,7 +40,7 @@ def tile_picked_ysph_col_p_kernel(tc, x_words, x_scales, w1, offs, out):
         scale_table = keep.tile([P, T], U8, name="scale_table", align_bytes=64)
         nc.gpsimd.memset(scale_table[:].bitcast(I32), 0)
         for q in range(4):
-            nc.gpsimd.dma_start(
+            nc.scalar.dma_start(
                 out=scale_table[32 * q : 32 * q + 8, :].bitcast(I32),
                 in_=x_scales[:, 4 * q : 4 * q + 4, :].bitcast(I32),
             )
@@ -55,23 +54,21 @@ def tile_picked_ysph_col_p_kernel(tc, x_words, x_scales, w1, offs, out):
                 in_=x_words[g].rearrange("p n t -> p (n t)").bitcast(I32),
             )
 
-        load_words(0)
         for g in range(PASSES):
             nc.sync.dma_start(out=w_raw[g][:], in_=w1[512 * g : 512 * (g + 1), :].rearrange("(p j) m -> p j m", j=4))
-        load_words(1)
+            load_words(g)
 
         ones = keep.tile([P, P], F32, name="ones")
-        nc.vector.memset(ones[:], 1.0)
+        nc.gpsimd.memset(ones[:], 1.0)
         warm = keep.tile([P, 1], F32, name="warm")
         nc.scalar.activation(warm[:], ones[:, 0:1], ACT.Abs_reciprocal_sqrt)
         floor = keep.tile([P, P], F32, name="floor")
         nc.vector.tensor_scalar(floor[:], ones[:], 0.6, None, ALU.mult)
         ident = keep.tile([P, P], F32, name="ident")
-        nc.vector.memset(ident[:], 0.0)
-        make_identity(nc, ident[:], nomemset=True)
+        make_identity(nc, ident[:])
 
         x_codes = [[keep.tile([P, PIECE], U32, name=f"x_codes{g}_{j}", align_bytes=64) for j in range(PIECES)] for g in range(PASSES)]
-        x_planes = [keep.tile([P, PIECE], U8, name="x_planes", align_bytes=64) for j in range(PIECES)]
+        x_planes = [keep.tile([P, PIECE], U8, name=f"x_planes{j}", align_bytes=64) for j in range(PIECES)]
 
         def piece(j):
             return offsets[:, j * PIECE // 16 : (j + 1) * PIECE // 16]
@@ -112,15 +109,17 @@ def tile_picked_ysph_col_p_kernel(tc, x_words, x_scales, w1, offs, out):
             )
 
         for j in range(PIECES):
-            gather_words(0, j)
-        for g in range(PASSES):
-            quantise_weights(g)
-        for j in range(PIECES):
             gather_scales(j)
+        quantise_weights(0)
+        for j in range(PIECES):
+            gather_words(0, j)
+        quantise_weights(1)
+        for c in range(CHUNKS):
+            product(c, 0)
+        for j in range(PIECES):
             gather_words(1, j)
             for h in range(HALVES):
-                for g in range(PASSES):
-                    product(j * HALVES + h, g)
+                product(j * HALVES + h, 1)
 
         dens_early = d_psum.tile([P, LAST, P], F32, name="dens_early")
         dens_last = d_psum.tile([P, P], F32, name="dens_last")
@@ -136,12 +135,12 @@ def tile_picked_ysph_col_p_kernel(tc, x_words, x_scales, w1, offs, out):
 
         def weights(c):
             neg = work.tile([P, D, P], F32, name="neg") if c < LAST else keep.tile([P, D, P], F32, name="late")
-            if c == 0:
-                nc.scalar.activation(neg[:], sq[c][:], ACT.Relu, scale=-1.0, bias=ones[:, 0:1])
-            else:
-                nc.vector.tensor_scalar(neg[:], sq[c][:], 1.0, 1.0, ALU.min, ALU.subtract)
+            nc.vector.tensor_scalar(neg[:], sq[c][:], 1.0, 1.0, ALU.min, ALU.subtract)
             ker[c] = work.tile([P, D, P], F32, name="ker")
-            nc.scalar.activation(ker[c][:], neg[:], ACT.Square)
+            if c == 0:
+                nc.vector.tensor_tensor(ker[c][:], neg[:], neg[:], ALU.mult)
+            else:
+                nc.scalar.activation(ker[c][:], neg[:], ACT.Square)
             if c < LAST:
                 for d in range(D):
                     turn(dens_early[:, c, :], ker[c][:, d, :], d == 0, d == D - 1)
@@ -153,7 +152,7 @@ def tile_picked_ysph_col_p_kernel(tc, x_words, x_scales, w1, offs, out):
         def gradient(c):
             wy = work.tile([P, D, P], F32, name="wy")
             nc.vector.tensor_tensor(wy[:], ker[c][:], by_pair[c], ALU.mult)
-            cf[c] = c_psum.tile([P, P], F32, name="cf")
+            cf[c] = y_psum.tile([P, P], F32, name="y")
             for d in range(D):
                 turn(cf[c][:], wy[:, d, :], d == 0, d == D - 1)
 
@@ -176,8 +175,8 @@ def tile_picked_ysph_col_p_kernel(tc, x_words, x_scales, w1, offs, out):
         square(0)
         square(1)
         weights(0)
-        square(2)
         weights(1)
+        square(2)
         square(3)
         gradient(0)
         inverse(0)
@@ -199,7 +198,8 @@ def tile_picked_ysph_col_p_kernel(tc, x_words, x_scales, w1, offs, out):
             turn(back[c][:], term[c][:], True, False)
 
         logd = keep.tile([P, CHUNKS, P], F32, name="late")
-        nc.scalar.activation(logd[:, 0:LAST, :], dens_early[:], ACT.Ln, bias=floor[:, 0:1])
+        for c in range(LAST):
+            nc.scalar.activation(logd[:, c, :], dens_early[:, c, :], ACT.Ln, bias=floor[:, 0:1])
         nc.scalar.activation(logd[:, LAST, :], inv[LAST][:], ACT.Ln)
         turn(back[LAST][:], logd[:, LAST, :], True, False)
         turn(back[LAST][:], term[LAST][:], False, True)

@@ -40,7 +40,7 @@ def tile_picked_ysph_col_p_kernel(tc, x_words, x_scales, w1, offs, out):
         scale_table = keep.tile([P, T], U8, name="scale_table", align_bytes=64)
         nc.gpsimd.memset(scale_table[:].bitcast(I32), 0)
         for q in range(4):
-            nc.scalar.dma_start(
+            nc.sync.dma_start(
                 out=scale_table[32 * q : 32 * q + 8, :].bitcast(I32),
                 in_=x_scales[:, 4 * q : 4 * q + 4, :].bitcast(I32),
             )
@@ -55,7 +55,9 @@ def tile_picked_ysph_col_p_kernel(tc, x_words, x_scales, w1, offs, out):
             )
 
         for g in range(PASSES):
-            nc.sync.dma_start(out=w_raw[g][:], in_=w1[512 * g : 512 * (g + 1), :].rearrange("(p j) m -> p j m", j=4))
+            w_rows = w1[512 * g : 512 * (g + 1), :].rearrange("(p j) m -> p j m", j=4)
+            for j0, j1 in ((0, 2), (2, 4)) if g == 0 else ((0, 4),):
+                nc.sync.dma_start(out=w_raw[g][:, j0:j1, :], in_=w_rows[:, j0:j1, :])
             load_words(g)
 
         ones = keep.tile([P, P], F32, name="ones")
@@ -123,38 +125,38 @@ def tile_picked_ysph_col_p_kernel(tc, x_words, x_scales, w1, offs, out):
 
         dens_early = d_psum.tile([P, LAST, P], F32, name="dens_early")
         dens_last = d_psum.tile([P, P], F32, name="dens_last")
-        by_pair = [y[c][:].rearrange("p (v d) -> p d v", d=D) for c in range(CHUNKS)]
+        by_pair = [y[c][:].rearrange("p (v a e) -> p a v e", a=2, e=2) for c in range(CHUNKS)]
         sq, ker, cf, inv, back, term = {}, {}, {}, {}, {}, {}
 
         def turn(dst, src, start, stop):
             nc.tensor.matmul(dst, lhsT=src, rhs=ident[:], start=start, stop=stop, is_transpose=True)
 
         def square(c):
-            sq[c] = work.tile([P, D, P], F32, name="sq")
+            sq[c] = work.tile([P, 2, P, 2], F32, name="sq")
             nc.scalar.activation(sq[c][:], by_pair[c], ACT.Square, scale=math.sqrt(0.2))
 
         def weights(c):
-            neg = work.tile([P, D, P], F32, name="neg") if c < LAST else keep.tile([P, D, P], F32, name="late")
+            neg = work.tile([P, 2, P, 2], F32, name="neg") if c < LAST else keep.tile([P, 2, P, 2], F32, name="late")
             nc.vector.tensor_scalar(neg[:], sq[c][:], 1.0, 1.0, ALU.min, ALU.subtract)
-            ker[c] = work.tile([P, D, P], F32, name="ker")
+            ker[c] = work.tile([P, 2, P, 2], F32, name="ker")
             if c == 0:
                 nc.vector.tensor_tensor(ker[c][:], neg[:], neg[:], ALU.mult)
             else:
                 nc.scalar.activation(ker[c][:], neg[:], ACT.Square)
             if c < LAST:
                 for d in range(D):
-                    turn(dens_early[:, c, :], ker[c][:, d, :], d == 0, d == D - 1)
+                    turn(dens_early[:, c, :], ker[c][:, d // 2, :, d % 2], d == 0, d == D - 1)
             else:
                 turn(dens_last[:], floor[:], True, False)
                 for d in range(D):
-                    turn(dens_last[:], ker[c][:, d, :], False, d == D - 1)
+                    turn(dens_last[:], ker[c][:, d // 2, :, d % 2], False, d == D - 1)
 
         def gradient(c):
-            wy = work.tile([P, D, P], F32, name="wy")
+            wy = work.tile([P, 2, P, 2], F32, name="wy")
             nc.vector.tensor_tensor(wy[:], ker[c][:], by_pair[c], ALU.mult)
             cf[c] = y_psum.tile([P, P], F32, name="y")
             for d in range(D):
-                turn(cf[c][:], wy[:, d, :], d == 0, d == D - 1)
+                turn(cf[c][:], wy[:, d // 2, :, d % 2], d == 0, d == D - 1)
 
         def inverse(c):
             inv[c] = work.tile([P, P], F32, name="inv")

@@ -18,12 +18,15 @@ ACT = mybir.ActivationFunctionType
 ALU = mybir.AluOpType
 
 P = 128
-PASSES = K // 512
+PACK = 4
+K_PASS = P * PACK
+PASSES = K // K_PASS
 HALVES = N // P
 PIECE = P * D
 PIECES = S // PIECE
 CHUNKS = PIECES * HALVES
 LAST = CHUNKS - 1
+SPARE_BANKS = 2
 
 
 def tile_picked_ysph_col_p_kernel(tc, x_words, x_scales, w1, offs, out):
@@ -31,46 +34,49 @@ def tile_picked_ysph_col_p_kernel(tc, x_words, x_scales, w1, offs, out):
     with ExitStack() as ctx:
         keep = ctx.enter_context(tc.tile_pool(name="keep", bufs=1))
         work = ctx.enter_context(tc.tile_pool(name="work", bufs=CHUNKS))
-        y_psum = ctx.enter_context(tc.psum_pool(name="y_psum", bufs=CHUNKS + 2))
-        d_psum = ctx.enter_context(tc.psum_pool(name="d_psum", bufs=1))
+        banks = ctx.enter_context(tc.psum_pool(name="banks", bufs=CHUNKS + SPARE_BANKS))
+        dens_banks = ctx.enter_context(tc.psum_pool(name="dens_banks", bufs=1))
 
         offsets = keep.tile([P, S // 16], U16, name="offsets")
         nc.sync.dma_start(offsets[:], offs)
 
         scale_table = keep.tile([P, T], U8, name="scale_table", align_bytes=64)
         nc.gpsimd.memset(scale_table[:].bitcast(I32), 0)
-        for q in range(4):
+        for q in range(P // 32):
             nc.sync.dma_start(
-                out=scale_table[32 * q : 32 * q + 8, :].bitcast(I32),
-                in_=x_scales[:, 4 * q : 4 * q + 4, :].bitcast(I32),
+                out=scale_table[32 * q : 32 * q + PASSES * PACK, :].bitcast(I32),
+                in_=x_scales[:, PACK * q : PACK * (q + 1), :].bitcast(I32),
             )
 
         word_table = [keep.tile([P, T], U32, name=f"word_table{g}", align_bytes=64) for g in range(PASSES)]
-        w_raw = [keep.tile([P, 4, N], F32, name=f"w_raw{g}") for g in range(PASSES)]
-
-        def load_words(g):
+        w_raw = [keep.tile([P, PACK, N], F32, name=f"w_raw{g}") for g in range(PASSES)]
+        for g in range(PASSES):
+            w_rows = w1[K_PASS * g : K_PASS * (g + 1), :].rearrange("(p t) m -> p t m", t=PACK)
+            t_step = PACK // 2 if g == 0 else PACK
+            for t in range(0, PACK, t_step):
+                nc.sync.dma_start(out=w_raw[g][:, t : t + t_step, :], in_=w_rows[:, t : t + t_step, :])
             nc.sync.dma_start(
                 out=word_table[g][:].bitcast(I32),
                 in_=x_words[g].rearrange("p n t -> p (n t)").bitcast(I32),
             )
 
-        for g in range(PASSES):
-            w_rows = w1[512 * g : 512 * (g + 1), :].rearrange("(p j) m -> p j m", j=4)
-            for j0, j1 in ((0, 2), (2, 4)) if g == 0 else ((0, 4),):
-                nc.sync.dma_start(out=w_raw[g][:, j0:j1, :], in_=w_rows[:, j0:j1, :])
-            load_words(g)
-
         ones = keep.tile([P, P], F32, name="ones")
         nc.gpsimd.memset(ones[:], 1.0)
-        warm = keep.tile([P, 1], F32, name="warm")
-        nc.scalar.activation(warm[:], ones[:, 0:1], ACT.Abs_reciprocal_sqrt)
+        root_015 = keep.tile([P, 1], F32, name="root_015")
+        nc.scalar.activation(root_015[:], ones[:, 0:1], ACT.Abs_reciprocal_sqrt, scale=1.0 / 0.15)
         floor = keep.tile([P, P], F32, name="floor")
         nc.vector.tensor_scalar(floor[:], ones[:], 0.6, None, ALU.mult)
         ident = keep.tile([P, P], F32, name="ident")
         make_identity(nc, ident[:])
 
-        x_codes = [[keep.tile([P, PIECE], U32, name=f"x_codes{g}_{j}", align_bytes=64) for j in range(PIECES)] for g in range(PASSES)]
+        x_codes = [
+            [keep.tile([P, PIECE], U32, name=f"x_codes{g}_{j}", align_bytes=64) for j in range(PIECES)]
+            for g in range(PASSES)
+        ]
         x_planes = [keep.tile([P, PIECE], U8, name=f"x_planes{j}", align_bytes=64) for j in range(PIECES)]
+        w_codes = [keep.tile([P, N], U32, name=f"w_codes{g}", align_bytes=64) for g in range(PASSES)]
+        w_planes = [keep.tile([P, N], U8, name=f"w_planes{g}", align_bytes=64) for g in range(PASSES)]
+        y = [banks.tile([P, PIECE], F32, name="bank") for c in range(CHUNKS)]
 
         def piece(j):
             return offsets[:, j * PIECE // 16 : (j + 1) * PIECE // 16]
@@ -78,40 +84,33 @@ def tile_picked_ysph_col_p_kernel(tc, x_words, x_scales, w1, offs, out):
         def gather_words(g, j):
             nc.vector.tensor_copy(x_codes[g][j][:], word_table[g][:].indirect(piece(j)))
 
-        def gather_scales(j):
-            nc.vector.tensor_copy(x_planes[j][:], scale_table[:].indirect(piece(j)))
-
-        w_codes, w_planes = [], []
-
         def quantise_weights(g):
-            grouped = keep.tile([P, N, 4], BF16, name=f"grouped{g}", align_bytes=64)
+            grouped = keep.tile([P, N, PACK], BF16, name=f"grouped{g}", align_bytes=64)
             nc.scalar.copy(
                 out=grouped[:].rearrange("p (c i) t -> p c t i", i=4),
                 in_=w_raw[g][:].rearrange("p t (c i) -> p c t i", i=4),
             )
-            codes = keep.tile([P, N], U32, name=f"w_codes{g}", align_bytes=64)
-            plane = keep.tile([P, N], U8, name=f"w_plane{g}", align_bytes=64)
-            nc.vector.quantize_mx(out=codes[:].bitcast(FP8X4), scales=plane[:], in_=grouped[:].rearrange("p m t -> p (m t)"))
-            w_codes.append(codes)
-            w_planes.append(plane)
-
-        y = [y_psum.tile([P, PIECE], F32, name="y") for c in range(CHUNKS)]
+            nc.vector.quantize_mx(
+                out=w_codes[g][:].bitcast(FP8X4),
+                scales=w_planes[g][:],
+                in_=grouped[:].rearrange("p m t -> p (m t)"),
+            )
 
         def product(c, g):
             j, h = divmod(c, HALVES)
-            cols = slice(h * P, (h + 1) * P)
+            rows = slice(h * P, (h + 1) * P)
             nc.tensor.matmul_mx(
                 out=y[c][:],
-                lhsT=w_codes[g][:, cols].bitcast(FP8X4),
-                lhsT_scale=w_planes[g][:, cols],
+                lhsT=w_codes[g][:, rows].bitcast(FP8X4),
+                lhsT_scale=w_planes[g][:, rows],
                 rhs=x_codes[g][j][:].bitcast(FP8X4),
-                rhs_scale=x_planes[j][4 * g : P, :],
+                rhs_scale=x_planes[j][PACK * g : P, :],
                 start=(g == 0),
                 stop=(g == PASSES - 1),
             )
 
         for j in range(PIECES):
-            gather_scales(j)
+            nc.vector.tensor_copy(x_planes[j][:], scale_table[:].indirect(piece(j)))
         quantise_weights(0)
         for j in range(PIECES):
             gather_words(0, j)
@@ -123,19 +122,23 @@ def tile_picked_ysph_col_p_kernel(tc, x_words, x_scales, w1, offs, out):
             for h in range(HALVES):
                 product(j * HALVES + h, 1)
 
-        dens_early = d_psum.tile([P, LAST, P], F32, name="dens_early")
-        dens_last = d_psum.tile([P, P], F32, name="dens_last")
-        by_pair = [y[c][:].rearrange("p (v a e) -> p a v e", a=2, e=2) for c in range(CHUNKS)]
-        sq, ker, cf, inv, back, term = {}, {}, {}, {}, {}, {}
+        y_pairs = [y[c][:].rearrange("p (v a e) -> p a v e", a=2, e=2) for c in range(CHUNKS)]
+        dens_early = dens_banks.tile([P, LAST, P], F32, name="dens_early")
+        dens_last = dens_banks.tile([P, P], F32, name="dens_last")
+        inv = keep.tile([P, CHUNKS, P], F32, name="inv")
+        sq, ker, cf, term = {}, {}, {}, {}
+
+        def member(tile, d):
+            return tile[:, d // 2, :, d % 2]
 
         def turn(dst, src, start, stop):
             nc.tensor.matmul(dst, lhsT=src, rhs=ident[:], start=start, stop=stop, is_transpose=True)
 
         def square(c):
             sq[c] = work.tile([P, 2, P, 2], F32, name="sq")
-            nc.scalar.activation(sq[c][:], by_pair[c], ACT.Square, scale=math.sqrt(0.2))
+            nc.scalar.activation(sq[c][:], y_pairs[c], ACT.Square, scale=math.sqrt(0.2))
 
-        def weights(c):
+        def density(c):
             neg = work.tile([P, 2, P, 2], F32, name="neg") if c < LAST else keep.tile([P, 2, P, 2], F32, name="late")
             nc.vector.tensor_scalar(neg[:], sq[c][:], 1.0, 1.0, ALU.min, ALU.subtract)
             ker[c] = work.tile([P, 2, P, 2], F32, name="ker")
@@ -145,74 +148,58 @@ def tile_picked_ysph_col_p_kernel(tc, x_words, x_scales, w1, offs, out):
                 nc.scalar.activation(ker[c][:], neg[:], ACT.Square)
             if c < LAST:
                 for d in range(D):
-                    turn(dens_early[:, c, :], ker[c][:, d // 2, :, d % 2], d == 0, d == D - 1)
+                    turn(dens_early[:, c, :], member(ker[c], d), d == 0, d == D - 1)
             else:
                 turn(dens_last[:], floor[:], True, False)
                 for d in range(D):
-                    turn(dens_last[:], ker[c][:, d // 2, :, d % 2], False, d == D - 1)
+                    turn(dens_last[:], member(ker[c], d), False, d == D - 1)
 
         def gradient(c):
             wy = work.tile([P, 2, P, 2], F32, name="wy")
-            nc.vector.tensor_tensor(wy[:], ker[c][:], by_pair[c], ALU.mult)
-            cf[c] = y_psum.tile([P, P], F32, name="y")
+            nc.vector.tensor_tensor(wy[:], ker[c][:], y_pairs[c], ALU.mult)
+            cf[c] = banks.tile([P, P], F32, name="bank")
             for d in range(D):
-                turn(cf[c][:], wy[:, d // 2, :, d % 2], d == 0, d == D - 1)
-
-        def inverse(c):
-            inv[c] = work.tile([P, P], F32, name="inv")
-            if c < LAST:
-                nc.scalar.activation(inv[c][:], dens_early[:, c, :], ACT.Abs_reciprocal_sqrt, bias=floor[:, 0:1])
-            else:
-                nc.vector.reciprocal(inv[c][:], dens_last[:])
+                turn(cf[c][:], member(wy, d), d == 0, d == D - 1)
 
         def gradient_term(c):
             scaled = work.tile([P, P], F32, name="scaled")
             term[c] = work.tile([P, P], F32, name="term")
-            nc.vector.tensor_tensor(scaled[:], cf[c][:], inv[c][:], ALU.mult)
-            if c < LAST:
-                nc.vector.scalar_tensor_tensor(term[c][:], scaled[:], -0.3, scaled[:], ALU.mult, ALU.mult)
+            nc.vector.tensor_tensor(scaled[:], cf[c][:], inv[:, c, :], ALU.mult)
+            if c < HALVES:
+                nc.scalar.activation(term[c][:], scaled[:], ACT.Square, scale=root_015[:])
+            elif c < LAST:
+                nc.vector.scalar_tensor_tensor(term[c][:], scaled[:], 0.15, scaled[:], ALU.mult, ALU.mult)
             else:
                 nc.vector.scalar_tensor_tensor(term[c][:], scaled[:], 0.3, cf[c][:], ALU.mult, ALU.mult)
 
-        square(0)
-        square(1)
-        weights(0)
-        weights(1)
-        square(2)
-        square(3)
-        gradient(0)
-        inverse(0)
-        weights(2)
-        weights(3)
-        gradient(1)
-        inverse(1)
-        inverse(2)
-        gradient_term(0)
-        gradient(2)
-        gradient_term(1)
-        gradient(3)
-        inverse(3)
-        gradient_term(3)
-        gradient_term(2)
-        for c in range(CHUNKS):
-            back[c] = y_psum.tile([P, P], F32, name="y")
-        for c in range(LAST):
-            turn(back[c][:], term[c][:], True, False)
-
-        logd = keep.tile([P, CHUNKS, P], F32, name="late")
-        for c in range(LAST):
-            nc.scalar.activation(logd[:, c, :], dens_early[:, c, :], ACT.Ln, bias=floor[:, 0:1])
-        nc.scalar.activation(logd[:, LAST, :], inv[LAST][:], ACT.Ln)
-        turn(back[LAST][:], logd[:, LAST, :], True, False)
-        turn(back[LAST][:], term[LAST][:], False, True)
-        for c in range(LAST):
-            turn(back[c][:], logd[:, c, :], False, True)
-
-        rows = out.rearrange("(h p) v -> p h v", p=P)
-        res = [keep.tile([P, HALVES, P], F32, name=f"res{j}") for j in range(PIECES)]
-        nc.vector.tensor_scalar(res[PIECES - 1][:, HALVES - 1, :], back[LAST][:], -1.0, None, ALU.mult)
-        for c in range(LAST):
-            j, h = divmod(c, HALVES)
-            nc.scalar.copy(out=res[j][:, h, :], in_=back[c][:])
         for j in range(PIECES):
-            nc.sync.dma_start(out=rows[:, :, j * P : (j + 1) * P], in_=res[j][:])
+            for h in range(HALVES):
+                square(j * HALVES + h)
+            for h in range(HALVES):
+                density(j * HALVES + h)
+
+        nc.scalar.activation(inv[:, 0:LAST, :], dens_early[:], ACT.Abs_reciprocal_sqrt, bias=floor[:, 0:1])
+        for c in range(CHUNKS):
+            gradient(c)
+        nc.vector.reciprocal(inv[:, LAST, :], dens_last[:])
+        for c in range(CHUNKS):
+            gradient_term(c)
+
+        total = [banks.tile([P, P], F32, name="bank") for c in range(CHUNKS)]
+        log_inv = keep.tile([P, CHUNKS, P], F32, name="late")
+        nc.scalar.activation(log_inv[:, 0:LAST, :], inv[:, 0:LAST, :], ACT.Ln)
+        nc.scalar.activation(log_inv[:, LAST, :], inv[:, LAST, :], ACT.Ln)
+        for c in range(CHUNKS):
+            turn(total[c][:], log_inv[:, c, :], True, False)
+        for c in range(CHUNKS):
+            turn(total[c][:], term[c][:], False, True)
+
+        for c in range(CHUNKS):
+            j, h = divmod(c, HALVES)
+            factor = -2.0 if c < LAST else -1.0
+            result = work.tile([P, P], F32, name="result")
+            if j == 0:
+                nc.vector.tensor_scalar(result[:], total[c][:], factor, None, ALU.mult)
+            else:
+                nc.scalar.activation(result[:], total[c][:], ACT.Copy, scale=factor)
+            nc.sync.dma_start(out=out[h * P : (h + 1) * P, j * P : (j + 1) * P], in_=result[:])

import math
from contextlib import ExitStack

import concourse.mybir as mybir
from concourse.masks import make_identity

K, T, S, D, N = 1024, 2048, 1024, 4, 256
FLOPS = 2 * K * N * S

F32 = mybir.dt.float32
BF16 = mybir.dt.bfloat16
I32 = mybir.dt.int32
U32 = mybir.dt.uint32
U16 = mybir.dt.uint16
U8 = mybir.dt.uint8
FP8X4 = mybir.dt.float8_e4m3fn_x4
ACT = mybir.ActivationFunctionType
ALU = mybir.AluOpType

P = 128
PACK = 4
K_PASS = P * PACK
PASSES = K // K_PASS
HALVES = N // P
PIECE = P * D
PIECES = S // PIECE
CHUNKS = PIECES * HALVES
LAST = CHUNKS - 1
SPARE_BANKS = 2


def tile_picked_ysph_col_p_kernel(tc, x_words, x_scales, w1, offs, out):
    nc = tc.nc
    with ExitStack() as ctx:
        keep = ctx.enter_context(tc.tile_pool(name="keep", bufs=1))
        work = ctx.enter_context(tc.tile_pool(name="work", bufs=CHUNKS))
        banks = ctx.enter_context(tc.psum_pool(name="banks", bufs=CHUNKS + SPARE_BANKS))
        dens_banks = ctx.enter_context(tc.psum_pool(name="dens_banks", bufs=1))

        offsets = keep.tile([P, S // 16], U16, name="offsets")
        nc.sync.dma_start(offsets[:], offs)

        scale_table = keep.tile([P, T], U8, name="scale_table", align_bytes=64)
        nc.gpsimd.memset(scale_table[:].bitcast(I32), 0)
        for q in range(P // 32):
            nc.sync.dma_start(
                out=scale_table[32 * q : 32 * q + PASSES * PACK, :].bitcast(I32),
                in_=x_scales[:, PACK * q : PACK * (q + 1), :].bitcast(I32),
            )

        word_table = [keep.tile([P, T], U32, name=f"word_table{g}", align_bytes=64) for g in range(PASSES)]
        w_raw = [keep.tile([P, PACK, N], F32, name=f"w_raw{g}") for g in range(PASSES)]
        for g in range(PASSES):
            w_rows = w1[K_PASS * g : K_PASS * (g + 1), :].rearrange("(p t) m -> p t m", t=PACK)
            t_step = PACK // 2 if g == 0 else PACK
            for t in range(0, PACK, t_step):
                nc.sync.dma_start(out=w_raw[g][:, t : t + t_step, :], in_=w_rows[:, t : t + t_step, :])
            nc.sync.dma_start(
                out=word_table[g][:].bitcast(I32),
                in_=x_words[g].rearrange("p n t -> p (n t)").bitcast(I32),
            )

        ones = keep.tile([P, P], F32, name="ones")
        nc.gpsimd.memset(ones[:], 1.0)
        root_015 = keep.tile([P, 1], F32, name="root_015")
        nc.scalar.activation(root_015[:], ones[:, 0:1], ACT.Abs_reciprocal_sqrt, scale=1.0 / 0.15)
        floor = keep.tile([P, P], F32, name="floor")
        nc.vector.tensor_scalar(floor[:], ones[:], 0.6, None, ALU.mult)
        ident = keep.tile([P, P], F32, name="ident")
        make_identity(nc, ident[:])

        x_codes = [
            [keep.tile([P, PIECE], U32, name=f"x_codes{g}_{j}", align_bytes=64) for j in range(PIECES)]
            for g in range(PASSES)
        ]
        x_planes = [keep.tile([P, PIECE], U8, name=f"x_planes{j}", align_bytes=64) for j in range(PIECES)]
        w_codes = [keep.tile([P, N], U32, name=f"w_codes{g}", align_bytes=64) for g in range(PASSES)]
        w_planes = [keep.tile([P, N], U8, name=f"w_planes{g}", align_bytes=64) for g in range(PASSES)]
        y = [banks.tile([P, PIECE], F32, name="bank") for c in range(CHUNKS)]

        def piece(j):
            return offsets[:, j * PIECE // 16 : (j + 1) * PIECE // 16]

        def gather_words(g, j):
            nc.vector.tensor_copy(x_codes[g][j][:], word_table[g][:].indirect(piece(j)))

        def quantise_weights(g):
            grouped = keep.tile([P, N, PACK], BF16, name=f"grouped{g}", align_bytes=64)
            nc.scalar.copy(
                out=grouped[:].rearrange("p (c i) t -> p c t i", i=4),
                in_=w_raw[g][:].rearrange("p t (c i) -> p c t i", i=4),
            )
            nc.vector.quantize_mx(
                out=w_codes[g][:].bitcast(FP8X4),
                scales=w_planes[g][:],
                in_=grouped[:].rearrange("p m t -> p (m t)"),
            )

        def product(c, g):
            j, h = divmod(c, HALVES)
            rows = slice(h * P, (h + 1) * P)
            nc.tensor.matmul_mx(
                out=y[c][:],
                lhsT=w_codes[g][:, rows].bitcast(FP8X4),
                lhsT_scale=w_planes[g][:, rows],
                rhs=x_codes[g][j][:].bitcast(FP8X4),
                rhs_scale=x_planes[j][PACK * g : P, :],
                start=(g == 0),
                stop=(g == PASSES - 1),
            )

        for j in range(PIECES):
            nc.vector.tensor_copy(x_planes[j][:], scale_table[:].indirect(piece(j)))
        quantise_weights(0)
        for j in range(PIECES):
            gather_words(0, j)
        quantise_weights(1)
        for c in range(CHUNKS):
            product(c, 0)
        for j in range(PIECES):
            gather_words(1, j)
            for h in range(HALVES):
                product(j * HALVES + h, 1)

        y_pairs = [y[c][:].rearrange("p (v a e) -> p a v e", a=2, e=2) for c in range(CHUNKS)]
        dens_early = dens_banks.tile([P, LAST, P], F32, name="dens_early")
        dens_last = dens_banks.tile([P, P], F32, name="dens_last")
        inv = keep.tile([P, CHUNKS, P], F32, name="inv")
        sq, ker, cf, term = {}, {}, {}, {}

        def member(tile, d):
            return tile[:, d // 2, :, d % 2]

        def turn(dst, src, start, stop):
            nc.tensor.matmul(dst, lhsT=src, rhs=ident[:], start=start, stop=stop, is_transpose=True)

        def square(c):
            sq[c] = work.tile([P, 2, P, 2], F32, name="sq")
            nc.scalar.activation(sq[c][:], y_pairs[c], ACT.Square, scale=math.sqrt(0.2))

        def density(c):
            neg = work.tile([P, 2, P, 2], F32, name="neg") if c < LAST else keep.tile([P, 2, P, 2], F32, name="late")
            nc.vector.tensor_scalar(neg[:], sq[c][:], 1.0, 1.0, ALU.min, ALU.subtract)
            ker[c] = work.tile([P, 2, P, 2], F32, name="ker")
            if c == 0:
                nc.vector.tensor_tensor(ker[c][:], neg[:], neg[:], ALU.mult)
            else:
                nc.scalar.activation(ker[c][:], neg[:], ACT.Square)
            if c < LAST:
                for d in range(D):
                    turn(dens_early[:, c, :], member(ker[c], d), d == 0, d == D - 1)
            else:
                turn(dens_last[:], floor[:], True, False)
                for d in range(D):
                    turn(dens_last[:], member(ker[c], d), False, d == D - 1)

        def gradient(c):
            wy = work.tile([P, 2, P, 2], F32, name="wy")
            nc.vector.tensor_tensor(wy[:], ker[c][:], y_pairs[c], ALU.mult)
            cf[c] = banks.tile([P, P], F32, name="bank")
            for d in range(D):
                turn(cf[c][:], member(wy, d), d == 0, d == D - 1)

        def gradient_term(c):
            scaled = work.tile([P, P], F32, name="scaled")
            term[c] = work.tile([P, P], F32, name="term")
            nc.vector.tensor_tensor(scaled[:], cf[c][:], inv[:, c, :], ALU.mult)
            if c < HALVES:
                nc.scalar.activation(term[c][:], scaled[:], ACT.Square, scale=root_015[:])
            elif c < LAST:
                nc.vector.scalar_tensor_tensor(term[c][:], scaled[:], 0.15, scaled[:], ALU.mult, ALU.mult)
            else:
                nc.vector.scalar_tensor_tensor(term[c][:], scaled[:], 0.3, cf[c][:], ALU.mult, ALU.mult)

        for j in range(PIECES):
            for h in range(HALVES):
                square(j * HALVES + h)
            for h in range(HALVES):
                density(j * HALVES + h)

        nc.scalar.activation(inv[:, 0:LAST, :], dens_early[:], ACT.Abs_reciprocal_sqrt, bias=floor[:, 0:1])
        for c in range(CHUNKS):
            gradient(c)
        nc.vector.reciprocal(inv[:, LAST, :], dens_last[:])
        for c in range(CHUNKS):
            gradient_term(c)

        total = [banks.tile([P, P], F32, name="bank") for c in range(CHUNKS)]
        log_inv = keep.tile([P, CHUNKS, P], F32, name="late")
        nc.scalar.activation(log_inv[:, 0:LAST, :], inv[:, 0:LAST, :], ACT.Ln)
        nc.scalar.activation(log_inv[:, LAST, :], inv[:, LAST, :], ACT.Ln)
        for c in range(CHUNKS):
            turn(total[c][:], log_inv[:, c, :], True, False)
        for c in range(CHUNKS):
            turn(total[c][:], term[c][:], False, True)

        for c in range(CHUNKS):
            j, h = divmod(c, HALVES)
            factor = -2.0 if c < LAST else -1.0
            result = work.tile([P, P], F32, name="result")
            if j == 0:
                nc.vector.tensor_scalar(result[:], total[c][:], factor, None, ALU.mult)
            else:
                nc.scalar.activation(result[:], total[c][:], ACT.Copy, scale=factor)
            nc.sync.dma_start(out=out[h * P : (h + 1) * P, j * P : (j + 1) * P], in_=result[:])
